import numpy as np
CORES = [3,11,19,27,35,43,51,59,67,75,83,91,99,107,115,123,131,139,147,155,163,171,179,187,195,203,211,219,227,235,243,251]
N = 32
WIDTHS = [1024 if r == 9 else 64 if r == 20 else 32 for r in range(N)]
WMAX = 1024
def setup_inputs(rng):
    return {"x": rng.standard_normal((N, 128, 2048), dtype=np.float32)}
def reference(x):
    s = x.sum(axis=0, dtype=np.float64).astype(x.dtype)
    y = np.full((N, 128, WMAX), np.nan, x.dtype)
    o = 0
    for r in range(N):
        y[r][:, :WIDTHS[r]] = s[:, o:o + WIDTHS[r]]
        o += WIDTHS[r]
    return {"y": y}

@@ -1,0 +1,85 @@
+from concourse.mybir import AluOpType
+
+SCRATCH = {
+    "lo": ("sbuf", [128, 32, 64], "float32"),
+    "lh": ("sbuf", [128, 32, 34], "float32"),
+    "xs": ("sbuf", [128, 2048], "float32"),
+    "l9": ("sbuf", [128, 1024], "float32"),
+}
+SEMAPHORES = ["ld", "own", "hot", "fin", "snt", "acc"]
+
+
+def plan(widths):
+    n = len(widths)
+    off = [sum(widths[:r]) for r in range(n)]
+    own = [(off[r], widths[r]) for r in range(n)]
+    own[9] = (off[9], 32)
+    hot = [None] * n
+    pos = off[9] + 32
+    k = 0
+    for r in range(n):
+        if r in (9, 20):
+            continue
+        w = 34 if k < 2 else 33
+        k += 1
+        hot[r] = (pos, w)
+        pos += w
+    return off, own, hot
+
+
+def rank_program(g, core, T, topo):
+    r = T.rank_of(core)
+    if r is None:
+        return
+    widths = T.tables["WIDTHS"]
+    off, own, hot = plan(widths)
+    n = len(widths)
+    S = T.sem
+    g.dma_start(T.xs[:], T.x[:]).then_inc(S.ld, 16)
+    o, w = own[r]
+    g.dma_start(T.lo[:, r, 0:w], T.x[:, o:o + w]).then_inc(S.ld, 16)
+    nld = 32
+    if hot[r]:
+        ho, hw = hot[r]
+        g.dma_start(T.lh[:, r, 0:hw], T.x[:, ho:ho + hw]).then_inc(S.ld, 16)
+        nld += 16
+    g.wait_ge(S.ld, nld)
+    sent = 0
+    for d in range(1, n):
+        q = (r + d) % n
+        dst = T.cores[q]
+        rid, pid = topo.addr(dst, core)
+        qo, qw = own[q]
+        g.remote_dma(T.lo[:, r, 0:qw], T.xs[:, qo:qo + qw], S.own, S.snt, pid, rid, 0xFF)
+        sent += 8
+        if hot[q]:
+            qo, qw = hot[q]
+            g.remote_dma(T.lh[:, r, 0:qw], T.xs[:, qo:qo + qw], S.hot, S.snt, pid, rid, 0xFF)
+            sent += 8
+    acc = 0
+    if hot[r]:
+        g.wait_ge(S.hot, 8 * (n - 1))
+        h = n // 2
+        while h >= 1:
+            g.dma_start(T.lh[:, 0:h, 0:hw], T.lh[:, h:2 * h, 0:hw], accum_op=AluOpType.add).then_inc(S.acc, 16)
+            acc += 16
+            g.wait_ge(S.acc, acc)
+            h //= 2
+        rid, pid = topo.addr(T.cores[9], core)
+        g.remote_dma(T.l9[:, ho - off[9]:ho - off[9] + hw], T.lh[:, 0, 0:hw], S.fin, S.snt, pid, rid, 0xFF)
+        sent += 8
+    g.wait_ge(S.own, 8 * (n - 1))
+    h = n // 2
+    while h >= 1:
+        g.dma_start(T.lo[:, 0:h, 0:w], T.lo[:, h:2 * h, 0:w], accum_op=AluOpType.add).then_inc(S.acc, 16)
+        acc += 16
+        g.wait_ge(S.acc, acc)
+        h //= 2
+    g.dma_start(T.y[:, 0:w], T.lo[:, 0, 0:w]).then_inc(S.acc, 16)
+    acc += 16
+    if r == 9:
+        g.wait_ge(S.fin, 8 * 30)
+        g.dma_start(T.y[:, 32:1024], T.l9[:, 32:1024]).then_inc(S.acc, 16)
+        acc += 16
+    g.wait_ge(S.acc, acc)
+    g.wait_ge(S.snt, sent)

@@ -1,85 +1,233 @@
+from concourse.bass import DstId, RemoteDMATransfer
 from concourse.mybir import AluOpType
 
+BW = 32
+NBLK = 64
+HOT0 = 9
+RC = 3
+WORKER = {(0, 0): {2: 2, 0: 0, 1: 4, 3: 5}, (1, 0): {3: 2, 0: 0, 1: 4, 2: 5},
+          (0, 1): {3: 2, 0: 0, 1: 4, 2: 5}, (1, 1): {0: 2, 3: 0, 1: 4, 2: 5}}
+EXTRA = (6, 2)
+
+
+def owner_rank(b):
+    if b < 9:
+        return b
+    if b < 41:
+        return 9
+    if b < 51:
+        return b - 31
+    if b < 53:
+        return 20
+    return b - 32
+
+
+def chip_of(h, p, k):
+    return h * 16 + 2 * k + p
+
+
+def block_info(b):
+    r = owner_rank(b)
+    if r != 9:
+        h, c = r // 16, r % 16
+        return (False, c % 2, c // 2, h, 3 if b == 52 else h, None)
+    j = b - HOT0
+    if j < 8:
+        return (True, 1, j, 0, 2, None)
+    if j < 16:
+        return (True, 1, j - 8, 1, 3, "chip8" if j - 8 == 4 else None)
+    if j == 16:
+        return (True, 1, 4, 0, 9, "chip8")
+    if j < 25:
+        return (True, 0, j - 17, 0, 2, None)
+    k = j - 25
+    return (True, 0, k if k < 2 else k + 1, 1, 3, None)
+
+
+def hub(ch, b):
+    return ch * 8 + (6 if b < 48 else 7)
+
+
+def worker(ch, b):
+    cls, special = block_info(b)[4:6]
+    if ch == 8 and special:
+        return 8 * 8 + 6
+    if cls == 9:
+        return ch * 8 + EXTRA[ch // 16]
+    return ch * 8 + WORKER[(ch // 16, ch % 2)][cls]
+
+
+def tree(b):
+    hot, p, k, f, cls, special = block_info(b)
+    own = owner_rank(b)
+    root = own * 8 + RC
+    par = {}
+    q = [8 if special else chip_of(0, p, k), chip_of(1, p, k)]
+    wq = [worker(q[0], b), worker(q[1], b)]
+    for h in (0, 1):
+        for kk in range(8):
+            cp, cm = chip_of(h, p, kk), chip_of(h, 1 - p, kk)
+            if hot and cp == 9:
+                par[8 * 8 + RC] = wq[0]
+                continue
+            w = worker(cp, b)
+            for c in (cp, cm):
+                if c == own:
+                    continue
+                if hot:
+                    par[c * 8 + RC] = w
+                else:
+                    par[c * 8 + RC] = hub(c, b)
+                    par[hub(c, b)] = w
+            if w != wq[h]:
+                par[w] = wq[h]
+    if hot:
+        par[wq[1 - f]] = wq[f]
+        par[wq[f]] = root
+    else:
+        par[wq[0]] = root
+        par[wq[1]] = root
+    return par
+
+
+def pow2floor(n):
+    v = 1
+    while v * 2 <= n:
+        v *= 2
+    return v
+
+
+def build():
+    par = {}
+    kids = {}
+    for b in range(NBLK):
+        for u, v in tree(b).items():
+            par[(u, b)] = v
+            kids.setdefault((v, b), []).append(u)
+    for key in kids:
+        kids[key].sort(key=lambda c: (c // 8 != key[0] // 8, c))
+    depth = {}
+
+    def dep(u, b):
+        if (u, b) not in depth:
+            depth[(u, b)] = 1 + max([dep(c, b) for c in kids.get((u, b), [])] + [0])
+        return depth[(u, b)]
+    for (u, b) in par:
+        dep(u, b)
+    lands = {}
+    for (v, b), cs in kids.items():
+        for c in cs:
+            lands.setdefault(v, []).append((c, b))
+    slot, size, layers = {}, {}, {}
+    for v, lst in lands.items():
+        if v % 8 == RC:
+            mine = sorted(set(b for c, b in lst))
+            w = len(mine) * BW
+            nl = len(kids[(v, mine[0])])
+            for b in mine:
+                for i, c in enumerate(kids[(v, b)]):
+                    slot[(v, c, b)] = i * w + (b - mine[0]) * BW
+            size[v] = nl * w
+            layers[v] = (nl, w)
+        else:
+            lst.sort()
+            for i, (c, b) in enumerate(lst):
+                slot[(v, c, b)] = i * BW
+            size[v] = len(lst) * BW
+    sends = {}
+    for (u, b), v in par.items():
+        sends.setdefault(u, []).append((depth[(u, b)], v, b))
+    prog, expect = {}, {}
+    for u, lst in sends.items():
+        lst.sort()
+        runs = []
+        for d, v, b in lst:
+            cs = kids.get((u, b), [])
+            srcs = [("x", b * BW)] if u % 8 == RC else [("l", slot[(u, c, b)]) for c in cs]
+            dst = slot[(v, u, b)]
+            if runs:
+                r = runs[-1]
+                if (r["d"] == d and r["v"] == v and r["kids"] == cs and r["dst"] + r["w"] == dst
+                        and all(s[1] + r["w"] == t[1] for s, t in zip(r["srcs"], srcs))):
+                    r["w"] += BW
+                    continue
+            runs.append({"d": d, "v": v, "kids": cs, "dst": dst, "w": BW, "srcs": srcs})
+        groups = {}
+        for r in runs:
+            groups.setdefault((r["d"], r["w"]), []).append(r)
+        calls = []
+        for (d, w) in sorted(groups):
+            off = [r for r in groups[(d, w)] if r["v"] // 8 != u // 8]
+            on = [r for r in groups[(d, w)] if r["v"] // 8 == u // 8]
+            while off or on:
+                a, off = off[:8], off[8:]
+                room = 8 if a else 16
+                c, on = on[:room], on[room:]
+                call = []
+                if a:
+                    e = pow2floor(8 // len(a))
+                    for i, r in enumerate(a):
+                        call.append((r, ((1 << e) - 1) << (i * e), e))
+                if c:
+                    e = pow2floor(room // len(c))
+                    for i, r in enumerate(c):
+                        call.append((r, ((1 << e) - 1) << ((8 if a else 0) + i * e), e))
+                calls.append((d, call))
+                for r, m, e in call:
+                    expect[(r["v"], d)] = expect.get((r["v"], d), 0) + e
+        prog[u] = calls
+    return {"prog": prog, "expect": expect, "size": size, "layers": layers, "maxd": max(depth.values())}
+
+
+PLAN = build()
+
 SCRATCH = {
-    "lo": ("sbuf", [128, 32, 64], "float32"),
-    "lh": ("sbuf", [128, 32, 34], "float32"),
-    "xs": ("sbuf", [128, 2048], "float32"),
-    "l9": ("sbuf", [128, 1024], "float32"),
+    "xs": ("sbuf", [128, NBLK * BW], "float32"),
+    "land": ("sbuf", [128, max(PLAN["size"].values())], "float32"),
 }
-SEMAPHORES = ["ld", "own", "hot", "fin", "snt", "acc"]
-
-
-def plan(widths):
-    n = len(widths)
-    off = [sum(widths[:r]) for r in range(n)]
-    own = [(off[r], widths[r]) for r in range(n)]
-    own[9] = (off[9], 32)
-    hot = [None] * n
-    pos = off[9] + 32
-    k = 0
-    for r in range(n):
-        if r in (9, 20):
-            continue
-        w = 34 if k < 2 else 33
-        k += 1
-        hot[r] = (pos, w)
-        pos += w
-    return off, own, hot
+SEMAPHORES = ["a1", "a2", "a3", "a4", "ld", "yi", "snt"]
 
 
 def rank_program(g, core, T, topo):
-    r = T.rank_of(core)
-    if r is None:
-        return
-    widths = T.tables["WIDTHS"]
-    off, own, hot = plan(widths)
-    n = len(widths)
     S = T.sem
-    g.dma_start(T.xs[:], T.x[:]).then_inc(S.ld, 16)
-    o, w = own[r]
-    g.dma_start(T.lo[:, r, 0:w], T.x[:, o:o + w]).then_inc(S.ld, 16)
-    nld = 32
-    if hot[r]:
-        ho, hw = hot[r]
-        g.dma_start(T.lh[:, r, 0:hw], T.x[:, ho:ho + hw]).then_inc(S.ld, 16)
-        nld += 16
-    g.wait_ge(S.ld, nld)
+    arrive = {1: S.a1, 2: S.a2, 3: S.a3, 4: S.a4}
+    calls = PLAN["prog"].get(core, [])
+    expect = PLAN["expect"]
+    rank = T.rank_of(core)
+    if rank is not None:
+        w = T.tables["WIDTHS"][rank]
+        o = sum(T.tables["WIDTHS"][:rank])
+        g.dma_start(T.xs[:], T.x[:]).then_inc(S.ld, 16)
+        g.dma_start(T.y[:, 0:w], T.x[:, o:o + w]).then_inc(S.yi, 16)
+        g.wait_ge(S.ld, 16)
+    waited = 0
     sent = 0
-    for d in range(1, n):
-        q = (r + d) % n
-        dst = T.cores[q]
-        rid, pid = topo.addr(dst, core)
-        qo, qw = own[q]
-        g.remote_dma(T.lo[:, r, 0:qw], T.xs[:, qo:qo + qw], S.own, S.snt, pid, rid, 0xFF)
-        sent += 8
-        if hot[q]:
-            qo, qw = hot[q]
-            g.remote_dma(T.lh[:, r, 0:qw], T.xs[:, qo:qo + qw], S.hot, S.snt, pid, rid, 0xFF)
-            sent += 8
-    acc = 0
-    if hot[r]:
-        g.wait_ge(S.hot, 8 * (n - 1))
-        h = n // 2
-        while h >= 1:
-            g.dma_start(T.lh[:, 0:h, 0:hw], T.lh[:, h:2 * h, 0:hw], accum_op=AluOpType.add).then_inc(S.acc, 16)
-            acc += 16
-            g.wait_ge(S.acc, acc)
-            h //= 2
-        rid, pid = topo.addr(T.cores[9], core)
-        g.remote_dma(T.l9[:, ho - off[9]:ho - off[9] + hw], T.lh[:, 0, 0:hw], S.fin, S.snt, pid, rid, 0xFF)
-        sent += 8
-    g.wait_ge(S.own, 8 * (n - 1))
-    h = n // 2
-    while h >= 1:
-        g.dma_start(T.lo[:, 0:h, 0:w], T.lo[:, h:2 * h, 0:w], accum_op=AluOpType.add).then_inc(S.acc, 16)
-        acc += 16
-        g.wait_ge(S.acc, acc)
-        h //= 2
-    g.dma_start(T.y[:, 0:w], T.lo[:, 0, 0:w]).then_inc(S.acc, 16)
-    acc += 16
-    if r == 9:
-        g.wait_ge(S.fin, 8 * 30)
-        g.dma_start(T.y[:, 32:1024], T.l9[:, 32:1024]).then_inc(S.acc, 16)
-        acc += 16
-    g.wait_ge(S.acc, acc)
-    g.wait_ge(S.snt, sent)
+    for d, call in calls:
+        while waited < d - 1:
+            waited += 1
+            if expect.get((core, waited)):
+                g.wait_ge(arrive[waited], expect[(core, waited)])
+        trs = []
+        for r, mask, e in call:
+            rid, pid = topo.addr(r["v"], core)
+            wd = r["w"]
+            srcs = [(T.xs if kind == "x" else T.land)[:, so:so + wd] for kind, so in r["srcs"]]
+            trs.append(RemoteDMATransfer(dst_ids=[DstId(rid=rid, pnc=pid)], dma_engine_mask=mask, remote_sem=arrive[d],
+                                         srcs=srcs, dsts=[T.land[:, r["dst"]:r["dst"] + wd]],
+                                         alu_op=1 if len(srcs) > 1 else 0))
+            sent += e
+        g.remote_dma_fused(trs, local_sem=S.snt)
+    while waited < PLAN["maxd"]:
+        waited += 1
+        if expect.get((core, waited)):
+            g.wait_ge(arrive[waited], expect[(core, waited)])
+    if rank is not None:
+        nl, w = PLAN["layers"][core]
+        done = 16
+        for i in range(nl):
+            g.wait_ge(S.yi, done)
+            g.dma_start(T.y[:, 0:w], T.land[:, i * w:(i + 1) * w], accum_op=AluOpType.add).then_inc(S.yi, 16)
+            done += 16
+        g.wait_ge(S.yi, done)
+    if sent:
+        g.wait_ge(S.snt, sent)

@@ -5,8 +5,9 @@ BW = 32
 NBLK = 64
 HOT0 = 9
 RC = 3
-WORKER = {(0, 0): {2: 2, 0: 0, 1: 4, 3: 5}, (1, 0): {3: 2, 0: 0, 1: 4, 2: 5},
-          (0, 1): {3: 2, 0: 0, 1: 4, 2: 5}, (1, 1): {0: 2, 3: 0, 1: 4, 2: 5}}
+WORKER = {(0, 0): {0: 2, 1: 0, 2: 4, 3: 5}, (1, 0): {0: 2, 1: 0, 2: 4, 3: 5},
+          (0, 1): {3: 2, 2: 0, 0: 4, 1: 5}, (1, 1): {0: 2, 3: 0, 1: 4, 2: 5}}
+DIRECT = 52
 EXTRA = (6, 2)
 
 
@@ -54,7 +55,15 @@ def worker(ch, b):
         return 8 * 8 + 6
     if cls == 9:
         return ch * 8 + EXTRA[ch // 16]
-    return ch * 8 + WORKER[(ch // 16, ch % 2)][cls]
+    c = WORKER[(ch // 16, ch % 2)][cls]
+    return ch * 8 + (1 if ch == 8 and c == 2 else c)
+
+
+def collector(ch, b):
+    hot, p, k, f, cls, special = block_info(b)
+    if hot and not special and p == 0 and ch // 16 == f:
+        return ch * 8 + (2 if ch == 8 else 7)
+    return worker(ch, b)
 
 
 def tree(b):
@@ -63,18 +72,22 @@ def tree(b):
     root = own * 8 + RC
     par = {}
     q = [8 if special else chip_of(0, p, k), chip_of(1, p, k)]
-    wq = [worker(q[0], b), worker(q[1], b)]
+    wq = [collector(q[0], b), collector(q[1], b)]
     for h in (0, 1):
         for kk in range(8):
             cp, cm = chip_of(h, p, kk), chip_of(h, 1 - p, kk)
             if hot and cp == 9:
-                par[8 * 8 + RC] = wq[0]
+                if wq[0] // 8 in (8, 9):
+                    par[8 * 8 + RC] = wq[0]
+                else:
+                    par[8 * 8 + RC] = 8 * 8 + 2
+                    par[8 * 8 + 2] = wq[0]
                 continue
             w = worker(cp, b)
             for c in (cp, cm):
                 if c == own:
                     continue
-                if hot:
+                if hot or b == DIRECT:
                     par[c * 8 + RC] = w
                 else:
                     par[c * 8 + RC] = hub(c, b)

from concourse.bass import DstId, RemoteDMATransfer
from concourse.mybir import AluOpType

BW = 32
NBLK = 64
HOT0 = 9
RC = 3
WORKER = {(0, 0): {0: 2, 1: 0, 2: 4, 3: 5}, (1, 0): {0: 2, 1: 0, 2: 4, 3: 5},
          (0, 1): {3: 2, 2: 0, 0: 4, 1: 5}, (1, 1): {0: 2, 3: 0, 1: 4, 2: 5}}
DIRECT = 52
EXTRA = (6, 2)


def owner_rank(b):
    if b < 9:
        return b
    if b < 41:
        return 9
    if b < 51:
        return b - 31
    if b < 53:
        return 20
    return b - 32


def chip_of(h, p, k):
    return h * 16 + 2 * k + p


def block_info(b):
    r = owner_rank(b)
    if r != 9:
        h, c = r // 16, r % 16
        return (False, c % 2, c // 2, h, 3 if b == 52 else h, None)
    j = b - HOT0
    if j < 8:
        return (True, 1, j, 0, 2, None)
    if j < 16:
        return (True, 1, j - 8, 1, 3, "chip8" if j - 8 == 4 else None)
    if j == 16:
        return (True, 1, 4, 0, 9, "chip8")
    if j < 25:
        return (True, 0, j - 17, 0, 2, None)
    k = j - 25
    return (True, 0, k if k < 2 else k + 1, 1, 3, None)


def hub(ch, b):
    return ch * 8 + (6 if b < 48 else 7)


def worker(ch, b):
    cls, special = block_info(b)[4:6]
    if ch == 8 and special:
        return 8 * 8 + 6
    if cls == 9:
        return ch * 8 + EXTRA[ch // 16]
    c = WORKER[(ch // 16, ch % 2)][cls]
    return ch * 8 + (1 if ch == 8 and c == 2 else c)


def collector(ch, b):
    hot, p, k, f, cls, special = block_info(b)
    if hot and not special and p == 0 and ch // 16 == f:
        return ch * 8 + (2 if ch == 8 else 7)
    return worker(ch, b)


def tree(b):
    hot, p, k, f, cls, special = block_info(b)
    own = owner_rank(b)
    root = own * 8 + RC
    par = {}
    q = [8 if special else chip_of(0, p, k), chip_of(1, p, k)]
    wq = [collector(q[0], b), collector(q[1], b)]
    for h in (0, 1):
        for kk in range(8):
            cp, cm = chip_of(h, p, kk), chip_of(h, 1 - p, kk)
            if hot and cp == 9:
                if wq[0] // 8 in (8, 9):
                    par[8 * 8 + RC] = wq[0]
                else:
                    par[8 * 8 + RC] = 8 * 8 + 2
                    par[8 * 8 + 2] = wq[0]
                continue
            w = worker(cp, b)
            for c in (cp, cm):
                if c == own:
                    continue
                if hot or b == DIRECT:
                    par[c * 8 + RC] = w
                else:
                    par[c * 8 + RC] = hub(c, b)
                    par[hub(c, b)] = w
            if w != wq[h]:
                par[w] = wq[h]
    if hot:
        par[wq[1 - f]] = wq[f]
        par[wq[f]] = root
    else:
        par[wq[0]] = root
        par[wq[1]] = root
    return par


def pow2floor(n):
    v = 1
    while v * 2 <= n:
        v *= 2
    return v


def build():
    par = {}
    kids = {}
    for b in range(NBLK):
        for u, v in tree(b).items():
            par[(u, b)] = v
            kids.setdefault((v, b), []).append(u)
    for key in kids:
        kids[key].sort(key=lambda c: (c // 8 != key[0] // 8, c))
    depth = {}

    def dep(u, b):
        if (u, b) not in depth:
            depth[(u, b)] = 1 + max([dep(c, b) for c in kids.get((u, b), [])] + [0])
        return depth[(u, b)]
    for (u, b) in par:
        dep(u, b)
    lands = {}
    for (v, b), cs in kids.items():
        for c in cs:
            lands.setdefault(v, []).append((c, b))
    slot, size, layers = {}, {}, {}
    for v, lst in lands.items():
        if v % 8 == RC:
            mine = sorted(set(b for c, b in lst))
            w = len(mine) * BW
            nl = len(kids[(v, mine[0])])
            for b in mine:
                for i, c in enumerate(kids[(v, b)]):
                    slot[(v, c, b)] = i * w + (b - mine[0]) * BW
            size[v] = nl * w
            layers[v] = (nl, w)
        else:
            lst.sort()
            for i, (c, b) in enumerate(lst):
                slot[(v, c, b)] = i * BW
            size[v] = len(lst) * BW
    sends = {}
    for (u, b), v in par.items():
        sends.setdefault(u, []).append((depth[(u, b)], v, b))
    prog, expect = {}, {}
    for u, lst in sends.items():
        lst.sort()
        runs = []
        for d, v, b in lst:
            cs = kids.get((u, b), [])
            srcs = [("x", b * BW)] if u % 8 == RC else [("l", slot[(u, c, b)]) for c in cs]
            dst = slot[(v, u, b)]
            if runs:
                r = runs[-1]
                if (r["d"] == d and r["v"] == v and r["kids"] == cs and r["dst"] + r["w"] == dst
                        and all(s[1] + r["w"] == t[1] for s, t in zip(r["srcs"], srcs))):
                    r["w"] += BW
                    continue
            runs.append({"d": d, "v": v, "kids": cs, "dst": dst, "w": BW, "srcs": srcs})
        groups = {}
        for r in runs:
            groups.setdefault((r["d"], r["w"]), []).append(r)
        calls = []
        for (d, w) in sorted(groups):
            off = [r for r in groups[(d, w)] if r["v"] // 8 != u // 8]
            on = [r for r in groups[(d, w)] if r["v"] // 8 == u // 8]
            while off or on:
                a, off = off[:8], off[8:]
                room = 8 if a else 16
                c, on = on[:room], on[room:]
                call = []
                if a:
                    e = pow2floor(8 // len(a))
                    for i, r in enumerate(a):
                        call.append((r, ((1 << e) - 1) << (i * e), e))
                if c:
                    e = pow2floor(room // len(c))
                    for i, r in enumerate(c):
                        call.append((r, ((1 << e) - 1) << ((8 if a else 0) + i * e), e))
                calls.append((d, call))
                for r, m, e in call:
                    expect[(r["v"], d)] = expect.get((r["v"], d), 0) + e
        prog[u] = calls
    return {"prog": prog, "expect": expect, "size": size, "layers": layers, "maxd": max(depth.values())}


PLAN = build()

SCRATCH = {
    "xs": ("sbuf", [128, NBLK * BW], "float32"),
    "land": ("sbuf", [128, max(PLAN["size"].values())], "float32"),
}
SEMAPHORES = ["a1", "a2", "a3", "a4", "ld", "yi", "snt"]


def rank_program(g, core, T, topo):
    S = T.sem
    arrive = {1: S.a1, 2: S.a2, 3: S.a3, 4: S.a4}
    calls = PLAN["prog"].get(core, [])
    expect = PLAN["expect"]
    rank = T.rank_of(core)
    if rank is not None:
        w = T.tables["WIDTHS"][rank]
        o = sum(T.tables["WIDTHS"][:rank])
        g.dma_start(T.xs[:], T.x[:]).then_inc(S.ld, 16)
        g.dma_start(T.y[:, 0:w], T.x[:, o:o + w]).then_inc(S.yi, 16)
        g.wait_ge(S.ld, 16)
    waited = 0
    sent = 0
    for d, call in calls:
        while waited < d - 1:
            waited += 1
            if expect.get((core, waited)):
                g.wait_ge(arrive[waited], expect[(core, waited)])
        trs = []
        for r, mask, e in call:
            rid, pid = topo.addr(r["v"], core)
            wd = r["w"]
            srcs = [(T.xs if kind == "x" else T.land)[:, so:so + wd] for kind, so in r["srcs"]]
            trs.append(RemoteDMATransfer(dst_ids=[DstId(rid=rid, pnc=pid)], dma_engine_mask=mask, remote_sem=arrive[d],
                                         srcs=srcs, dsts=[T.land[:, r["dst"]:r["dst"] + wd]],
                                         alu_op=1 if len(srcs) > 1 else 0))
            sent += e
        g.remote_dma_fused(trs, local_sem=S.snt)
    while waited < PLAN["maxd"]:
        waited += 1
        if expect.get((core, waited)):
            g.wait_ge(arrive[waited], expect[(core, waited)])
    if rank is not None:
        nl, w = PLAN["layers"][core]
        done = 16
        for i in range(nl):
            g.wait_ge(S.yi, done)
            g.dma_start(T.y[:, 0:w], T.land[:, i * w:(i + 1) * w], accum_op=AluOpType.add).then_inc(S.yi, 16)
            done += 16
        g.wait_ge(S.yi, done)
    if sent:
        g.wait_ge(S.snt, sent)
